import numpy as np
import ml_dtypes

BF16 = ml_dtypes.bfloat16


def bf(x):
    return np.asarray(x, np.float32).astype(BF16)


def f32(x):
    return np.asarray(x, np.float32)


def f64(x):
    return np.asarray(x).astype(np.float64)


def striped(idx):
    return np.concatenate([l.reshape(-1, 16).T for l in idx])


def rows(idx, k):
    return np.tile(np.repeat(idx, 16, axis=0), (k // (16 * 8), 1))


def look(tab, idx):
    return np.take_along_axis(f64(tab), rows(idx, len(tab)), axis=1)


K, S, V, N = 128, 2048, 1536, 1536


def setup_inputs():
    return {"tab": f32(np.random.standard_normal((2, K, S))), "y": f32(np.random.standard_normal((K, V))), "offs": striped(np.stack([np.random.permutation(S)[:N] for _ in range(8)]))}


def reference(tab, y, offs):
    idx = np.stack([g.T.reshape(-1) for g in np.split(offs, 8)])
    x = (np.minimum(look(tab[0], idx), f64(y))) * (1.0 / (1.0 + np.exp(-look(tab[1], idx))))
    return x

@@ -1,0 +1,38 @@
+import concourse.mybir as mybir
+
+F32, U16 = mybir.dt.float32, mybir.dt.uint16
+SIGMOID = mybir.ActivationFunctionType.Sigmoid
+MIN, MULT = mybir.AluOpType.min, mybir.AluOpType.mult
+
+PIECE = 512
+
+
+def tile_lookup_vg_minsig_out_kernel(tc, tab, y, offs, out):
+    nc = tc.nc
+    rows, places = tab.shape[1], tab.shape[2]
+    entries = y.shape[1]
+    pieces = range(entries // PIECE)
+
+    with tc.tile_pool(name="held", bufs=1) as held:
+        lists = held.tile([rows, entries // 16], U16, name="lists")
+        values = held.tile([rows, places], F32, name="values")
+        stream = held.tile([rows, entries], F32, name="stream")
+        gates = held.tile([rows, places], F32, name="gates")
+        nc.sync.dma_start(lists[:], offs)
+        nc.sync.dma_start(values[:], tab[0])
+        nc.sync.dma_start(stream[:], y)
+        nc.sync.dma_start(gates[:], tab[1])
+
+        smaller = [held.tile([rows, PIECE], F32, name=f"smaller{p}") for p in pieces]
+        opened = [held.tile([rows, PIECE], F32, name=f"opened{p}") for p in pieces]
+        product = [held.tile([rows, PIECE], F32, name=f"product{p}") for p in pieces]
+
+        for p in pieces:
+            columns = slice(p * PIECE, (p + 1) * PIECE)
+            offsets = lists[:, p * PIECE // 16 : (p + 1) * PIECE // 16]
+            nc.vector.tensor_tensor(smaller[p][:], values[:].indirect(offsets), stream[:, columns], MIN)
+            nc.scalar.activation(opened[p][:], gates[:].indirect(offsets), SIGMOID)
+
+        for p in pieces:
+            nc.vector.tensor_tensor(product[p][:], smaller[p][:], opened[p][:], MULT)
+            nc.sync.dma_start(out[:, p * PIECE : (p + 1) * PIECE], product[p][:])

@@ -23,6 +23,11 @@ def tile_lookup_vg_minsig_out_kernel(tc, tab, y, offs, out):
         nc.sync.dma_start(stream[:], y)
         nc.sync.dma_start(gates[:], tab[1])
 
+        zero = held.tile([rows, 1], F32, name="zero")
+        half = held.tile([rows, 1], F32, name="half")
+        nc.vector.memset(zero[:], 0.0)
+        nc.scalar.activation(half[:], zero[:], SIGMOID)
+
         smaller = [held.tile([rows, PIECE], F32, name=f"smaller{p}") for p in pieces]
         opened = [held.tile([rows, PIECE], F32, name=f"opened{p}") for p in pieces]
         product = [held.tile([rows, PIECE], F32, name=f"product{p}") for p in pieces]

@@ -16,12 +16,14 @@ def tile_lookup_vg_minsig_out_kernel(tc, tab, y, offs, out):
     with tc.tile_pool(name="held", bufs=1) as held:
         lists = held.tile([rows, entries // 16], U16, name="lists")
         values = held.tile([rows, places], F32, name="values")
-        stream = held.tile([rows, entries], F32, name="stream")
+        stream = [held.tile([rows, PIECE], F32, name=f"stream{p}") for p in pieces]
         gates = held.tile([rows, places], F32, name="gates")
         nc.sync.dma_start(lists[:], offs)
         nc.sync.dma_start(values[:], tab[0])
-        nc.sync.dma_start(stream[:], y)
+        nc.sync.dma_start(stream[0][:], y[:, :PIECE])
         nc.sync.dma_start(gates[:], tab[1])
+        for p in pieces[1:]:
+            nc.sync.dma_start(stream[p][:], y[:, p * PIECE : (p + 1) * PIECE])
 
         zero = held.tile([rows, 1], F32, name="zero")
         half = held.tile([rows, 1], F32, name="half")
@@ -33,9 +35,8 @@ def tile_lookup_vg_minsig_out_kernel(tc, tab, y, offs, out):
         product = [held.tile([rows, PIECE], F32, name=f"product{p}") for p in pieces]
 
         for p in pieces:
-            columns = slice(p * PIECE, (p + 1) * PIECE)
             offsets = lists[:, p * PIECE // 16 : (p + 1) * PIECE // 16]
-            nc.vector.tensor_tensor(smaller[p][:], values[:].indirect(offsets), stream[:, columns], MIN)
+            nc.vector.tensor_tensor(smaller[p][:], values[:].indirect(offsets), stream[p][:], MIN)
             nc.scalar.activation(opened[p][:], gates[:].indirect(offsets), SIGMOID)
 
         for p in pieces:

@@ -40,5 +40,10 @@ def tile_lookup_vg_minsig_out_kernel(tc, tab, y, offs, out):
             nc.scalar.activation(opened[p][:], gates[:].indirect(offsets), SIGMOID)
 
         for p in pieces:
-            nc.vector.tensor_tensor(product[p][:], smaller[p][:], opened[p][:], MULT)
-            nc.sync.dma_start(out[:, p * PIECE : (p + 1) * PIECE], product[p][:])
+            parts = 2 if p == pieces[-1] else 1
+            width = PIECE // parts
+            for part in range(parts):
+                columns = slice(part * width, (part + 1) * width)
+                first = p * PIECE + part * width
+                nc.vector.tensor_tensor(product[p][:, columns], smaller[p][:, columns], opened[p][:, columns], MULT)
+                nc.sync.dma_start(out[:, first : first + width], product[p][:, columns])

import concourse.mybir as mybir

F32, U16 = mybir.dt.float32, mybir.dt.uint16
SIGMOID = mybir.ActivationFunctionType.Sigmoid
MIN, MULT = mybir.AluOpType.min, mybir.AluOpType.mult

PIECE = 512


def tile_lookup_vg_minsig_out_kernel(tc, tab, y, offs, out):
    nc = tc.nc
    rows, places = tab.shape[1], tab.shape[2]
    entries = y.shape[1]
    pieces = range(entries // PIECE)

    with tc.tile_pool(name="held", bufs=1) as held:
        lists = held.tile([rows, entries // 16], U16, name="lists")
        values = held.tile([rows, places], F32, name="values")
        stream = [held.tile([rows, PIECE], F32, name=f"stream{p}") for p in pieces]
        gates = held.tile([rows, places], F32, name="gates")
        nc.sync.dma_start(lists[:], offs)
        nc.sync.dma_start(values[:], tab[0])
        nc.sync.dma_start(stream[0][:], y[:, :PIECE])
        nc.sync.dma_start(gates[:], tab[1])
        for p in pieces[1:]:
            nc.sync.dma_start(stream[p][:], y[:, p * PIECE : (p + 1) * PIECE])

        zero = held.tile([rows, 1], F32, name="zero")
        half = held.tile([rows, 1], F32, name="half")
        nc.vector.memset(zero[:], 0.0)
        nc.scalar.activation(half[:], zero[:], SIGMOID)

        smaller = [held.tile([rows, PIECE], F32, name=f"smaller{p}") for p in pieces]
        opened = [held.tile([rows, PIECE], F32, name=f"opened{p}") for p in pieces]
        product = [held.tile([rows, PIECE], F32, name=f"product{p}") for p in pieces]

        for p in pieces:
            offsets = lists[:, p * PIECE // 16 : (p + 1) * PIECE // 16]
            nc.vector.tensor_tensor(smaller[p][:], values[:].indirect(offsets), stream[p][:], MIN)
            nc.scalar.activation(opened[p][:], gates[:].indirect(offsets), SIGMOID)

        for p in pieces:
            parts = 2 if p == pieces[-1] else 1
            width = PIECE // parts
            for part in range(parts):
                columns = slice(part * width, (part + 1) * width)
                first = p * PIECE + part * width
                nc.vector.tensor_tensor(product[p][:, columns], smaller[p][:, columns], opened[p][:, columns], MULT)
                nc.sync.dma_start(out[:, first : first + width], product[p][:, columns])
